import numpy as np
import ml_dtypes


def mxq(x, axis, fmt="e4m3"):
    dtype, down = {"e4m3": (ml_dtypes.float8_e4m3fn, 7), "e5m2": (ml_dtypes.float8_e5m2, 14)}[fmt]
    v = np.moveaxis(np.asarray(x, np.float32).astype(ml_dtypes.bfloat16).astype(np.float64), axis, -1)
    blocks = v.reshape(v.shape[:-1] + (-1, 32))
    amax = np.abs(blocks).max(-1, keepdims=True)
    byte = np.maximum(np.where(amax > 0, np.frexp(amax)[1] - 1 + 127, 0) - down, 1)
    scale = np.exp2(byte - 127.0)
    codes = (blocks / scale).astype(np.float32).astype(dtype).astype(np.float64)
    return np.moveaxis((codes * scale).reshape(v.shape), -1, axis)


WIDE = False


def mx_kscale(k):
    if not WIDE:
        return np.ones(k)
    levels = np.array([10, -10, 5, -5, 0])
    if k % 512:
        return np.exp2(np.random.permutation(np.resize(levels, k // 32))).repeat(32)
    a = np.empty((k // 512, 16))
    for p in range(k // 512):
        a[p, :8] = np.random.permutation(np.resize(levels, 8))
        for g in range(8):
            far = levels[np.abs(levels - a[p, g]) >= 10]
            a[p, g + 8] = far[np.random.randint(len(far))]
    return np.exp2(a.ravel()).repeat(32)


def f64(x):
    return np.asarray(x).astype(np.float64)


def striped(idx):
    return np.tile(idx.reshape(-1, 16).T, (8, 1)).astype(np.uint16)


def unstriped(offs):
    return offs[:16].T.reshape(-1).astype(np.int64)


E2M1 = np.array([0.0, 0.5, 1.0, 1.5, 2.0, 3.0, 4.0, 6.0, -0.0, -0.5, -1.0, -1.5, -2.0, -3.0, -4.0, -6.0])


def pack_weight(w, fmt):
    k, n = w.shape
    w = f64(np.asarray(w, np.float32).astype(ml_dtypes.bfloat16)).reshape(k // 32, 32, n)
    amax = np.abs(w).max(1)
    if fmt == "e4m3":
        byte = np.frexp(amax)[1] - 1 + 127 - 7
    else:
        mant, ex = np.frexp(amax / 6.0)
        byte = np.where(mant > 0.5, ex, ex - 1) + 127
    byte = np.clip(np.where(amax > 0, byte, 1), 1, 254)
    scaled = (w * np.exp2(127.0 - byte)[:, None, :]).reshape(k, n).astype(np.float32)
    by_word = np.ascontiguousarray(scaled.reshape(k // 512, 128, 4, n).transpose(0, 1, 3, 2))
    if fmt == "e4m3":
        words = by_word.astype(ml_dtypes.float8_e4m3fn).view(np.uint8)
    else:
        c = by_word.astype(ml_dtypes.float4_e2m1fn).view(np.uint8) & 0xF
        words = (c[..., 0::2] | (c[..., 1::2] << 4)).reshape(k // 512, 128, 2 * n)
    return np.ascontiguousarray(words), np.ascontiguousarray(byte.astype(np.uint8).reshape(k // 512, 16, n))


def unpack_weight(words, scales, fmt):
    g, _, n = scales.shape
    words = np.ascontiguousarray(words).reshape(g, 128, n, -1)
    if fmt == "e4m3":
        vals = words.view(ml_dtypes.float8_e4m3fn).astype(np.float64)
    else:
        nib = np.empty((g, 128, n, 4), np.uint8)
        nib[..., 0::2] = words & 0xF
        nib[..., 1::2] = words >> 4
        vals = E2M1[nib]
    vals = vals * np.repeat(np.exp2(scales.astype(np.float64) - 127.0), 8, axis=1)[..., None]
    return vals.transpose(0, 1, 3, 2).reshape(g * 512, n)


def sigmoid(v):
    return 1.0 / (1.0 + np.exp(-np.maximum(v, -700.0)))


def d_sigmoid(v):
    s = 1.0 / (1.0 + np.exp(-np.maximum(v, -700.0)))
    return s * (1.0 - s)


K, T, E, C, H, N = 128, 1024, 6, 128, 512, 1536


def by_expert(wq, xq):
    return np.concatenate([wq[e].T @ xq[:, e * C:(e + 1) * C] for e in range(E)], axis=1)


def setup_inputs():
    n = np.random.standard_normal
    s = mx_kscale(N)[:, None]
    u = mx_kscale(H)
    dy = pack_weight(n((N, T)) * s, "e4m3")
    return {
        "dy_words": dy[0],
        "dy_scales": dy[1],
        "a1": n((H, E * C)).astype(np.float32),
        "a3": n((H, E * C)).astype(np.float32),
        "w2": (n((E, N, H)) / np.sqrt(N) / s[None] * u[None, None, :]).astype(np.float32),
        "w1": (n((E, H, K)) / np.sqrt(H) / u[None, :, None]).astype(np.float32),
        "w3": (n((E, H, K)) / np.sqrt(H) / u[None, :, None]).astype(np.float32),
        "gate": np.tile(np.random.uniform(0.2, 1.0, E * C), (H, 1)).astype(np.float32),
        "offs": striped(np.random.permutation(T)[:E * C]),
    }


def reference(dy_words, dy_scales, a1, a3, w2, w1, w3, gate, offs):
    idx = unstriped(offs)
    gq = unpack_weight(dy_words, dy_scales, "e4m3")[:, idx]
    dh = f64(gate) * by_expert(mxq(f64(w2), 1, "e4m3"), gq)
    da1 = dh * f64(a3) * d_sigmoid(f64(a1))
    da3 = dh * sigmoid(f64(a1))
    dx = by_expert(mxq(f64(w1), 1, "e4m3"), mxq(da1, 0, "e4m3")) + by_expert(mxq(f64(w3), 1, "e4m3"), mxq(da3, 0, "e4m3"))
    out = np.zeros((K, T))
    out[:, idx] = dx
    return out

@@ -1,0 +1,223 @@
+from contextlib import ExitStack
+
+import concourse.mybir as mybir
+from concourse.masks import make_identity
+
+K, T, E, C, H, N = 128, 1024, 6, 128, 512, 1536
+S = E * C
+FLOPS = 2 * S * (N * H + 2 * H * K)
+
+F32 = mybir.dt.float32
+BF16 = mybir.dt.bfloat16
+I32 = mybir.dt.int32
+U32 = mybir.dt.uint32
+U16 = mybir.dt.uint16
+U8 = mybir.dt.uint8
+FP8X4 = mybir.dt.float8_e4m3fn_x4
+ACT = mybir.ActivationFunctionType
+MULT = mybir.AluOpType.mult
+
+P = 128
+PACK = 4
+K_PASS = P * PACK
+PASSES = N // K_PASS
+RING = 12
+SCALAR_COLS = 320
+SCALAR_COLS_LAST = 192
+EARLY = 2
+
+
+def tile_moe_bdx_glu_sigmoid_kernel(
+    tc, dy_words, dy_scales, a1, a3, w2, w1, w3, gate, offs, out
+):
+    nc = tc.nc
+    with ExitStack() as ctx:
+        held = ctx.enter_context(tc.tile_pool(name="held", bufs=1))
+        ring = ctx.enter_context(tc.tile_pool(name="ring", bufs=RING))
+        work = ctx.enter_context(tc.tile_pool(name="work", bufs=2))
+        psum = ctx.enter_context(tc.psum_pool(name="psum", bufs=2))
+
+        offsets = held.tile([P, S // 16], U16, name="offsets")
+        nc.sync.dma_start(offsets[:], offs)
+
+        scale_rows = held.tile([P, T // 4], I32, name="scale_rows")
+        for q in range(4):
+            nc.scalar.dma_start(
+                scale_rows[32 * q : 32 * q + 4 * PASSES, :], dy_scales[:, 4 * q : 4 * q + 4, :].bitcast(I32)
+            )
+        gate_row = held.tile([E, C], F32, name="gate_row")
+        nc.scalar.dma_start(gate_row[:], gate[0:1, :].rearrange("o (e c) -> (o e) c", e=E))
+
+        dy_plane = held.tile([P, T], U8, name="dy_plane", align_bytes=64)
+        nc.vector.memset(dy_plane[:].bitcast(I32), 0)
+        for q in range(4):
+            live = slice(32 * q, 32 * q + 4 * PASSES)
+            nc.vector.tensor_copy(dy_plane[live, :].bitcast(I32), scale_rows[live, :])
+        gate_rows = held.tile([P, C], F32, name="gate_rows")
+        nc.gpsimd.memset(gate_rows[:], 0.0)
+        ident = held.tile([P, P], F32, name="ident")
+        make_identity(nc, ident[:])
+        window = held.tile([P, T], F32, name="window")
+        nc.gpsimd.memset(window[:], 0.0)
+        nc.vector.tensor_copy(gate_rows[0:E, :], gate_row[:])
+
+        dy_tiles = {}
+        w2_raw = {}
+        w13_raw = {}
+
+        def load_dy(o):
+            dy_tiles[o] = held.tile([P, T], I32, name="dy%d" % o, align_bytes=64)
+            nc.sync.dma_start(dy_tiles[o][:], dy_words[o].rearrange("p n t -> p (n t)").bitcast(I32))
+
+        def load_w2(e, o):
+            w2_raw[e, o] = ring.tile([P, PACK, H], F32, name="w2_raw", tag="raw")
+            nc.sync.dma_start(
+                w2_raw[e, o][:], w2[e, o * K_PASS : (o + 1) * K_PASS, :].rearrange("(p j) i -> p j i", j=PACK)
+            )
+
+        def load_w13(e):
+            w13_raw[e] = ring.tile([P, 2, PACK, K], F32, name="w13_raw", tag="raw")
+            for m, w in enumerate((w1, w3)):
+                nc.sync.dma_start(w13_raw[e][:, m], w[e].rearrange("(q t) k -> q t k", t=PACK))
+
+        a1_sb = held.tile([P, PACK, S], F32, name="a1_sb")
+        a3_sb = held.tile([P, PACK, S], F32, name="a3_sb")
+
+        def load_a(tile, a):
+            nc.sync.dma_start(tile[:], a.rearrange("(q t) s -> q t s", t=PACK))
+
+        g_words = {}
+        g_plane = held.tile([P, S], U8, name="g_plane", align_bytes=64)
+
+        def gather_words(o):
+            g_words[o] = held.tile([P, S], U32, name="g_words%d" % o, align_bytes=64)
+            nc.vector.tensor_copy(g_words[o][:], dy_tiles[o][:].bitcast(U32).indirect(offsets[:]))
+
+        def interleave(engine_copy, dst, src):
+            engine_copy(
+                dst.rearrange("p (c i) j -> p c j i", i=4),
+                src.rearrange("p j (c i) -> p c j i", i=4),
+            )
+
+        def quantize(grouped, words, tag, bufs):
+            codes = work.tile([P, words], U32, name=tag + "_codes", tag=tag + "_codes", bufs=bufs, align_bytes=64)
+            plane = work.tile([P, words], U8, name=tag + "_plane", tag=tag + "_plane", bufs=bufs, align_bytes=64)
+            nc.vector.quantize_mx(out=codes[:].bitcast(FP8X4), scales=plane[:], in_=grouped)
+            return codes, plane
+
+        gate_cols = held.tile([P, E], F32, name="gate_cols")
+
+        def turn_gate():
+            gate_ps = psum.tile([P, P], F32, name="gate_ps", tag="dx_ps")
+            nc.tensor.transpose(gate_ps[:], gate_rows[:], ident[:])
+            nc.vector.tensor_copy(gate_cols[:], gate_ps[:, 0:E])
+
+        dh_ps = {}
+
+        def first_pass(e, o):
+            grouped = work.tile([P, H, PACK], BF16, name="w2_bf", bufs=3, align_bytes=64)
+            raw = w2_raw[e, o]
+            cut = SCALAR_COLS_LAST if (e, o) == (E - 1, PASSES - 1) else SCALAR_COLS
+            interleave(nc.scalar.copy, grouped[:, :cut, :], raw[:, :, :cut])
+            interleave(nc.vector.tensor_copy, grouped[:, cut:, :], raw[:, :, cut:])
+            codes, plane = quantize(grouped[:].rearrange("p i j -> p (i j)"), H, "w2", 4)
+            if o == 0:
+                dh_ps[e] = psum.tile([P, H], F32, name="dh_ps", tag="dh_ps")
+            slots = slice(e * C, (e + 1) * C)
+            nc.tensor.matmul_mx(
+                out=dh_ps[e][:],
+                lhsT=g_words[o][:, slots].bitcast(FP8X4),
+                lhsT_scale=g_plane[4 * o :, slots],
+                rhs=codes[:].bitcast(FP8X4),
+                rhs_scale=plane[:],
+                start=(o == 0),
+                stop=(o == PASSES - 1),
+            )
+
+        factors = {}
+
+        def make_factors(e):
+            slots = slice(e * C, (e + 1) * C)
+            sig = work.tile([P, C, PACK], F32, name="sig", bufs=E)
+            slope = work.tile([P, C, PACK], F32, name="slope", bufs=E)
+            a1_e = a1_sb[:, :, slots].rearrange("q t s -> q s t")
+            nc.scalar.activation(sig[:], a1_e, ACT.Sigmoid)
+            nc.scalar.activation(slope[:], a1_e, ACT.Sigmoid, scale=-1.0)
+            nc.vector.tensor_tensor(slope[:], slope[:], a3_sb[:, :, slots].rearrange("q t s -> q s t"), MULT)
+            factors[e] = (sig, slope)
+
+        da_mx = {}
+
+        def middle(e):
+            sig, slope = factors[e]
+            dh_sb = work.tile([P, PACK, P], F32, name="dh_sb")
+            nc.scalar.activation(
+                dh_sb[:], dh_ps[e][:].rearrange("s (q t) -> s t q", t=PACK), ACT.Copy, scale=gate_cols[:, e : e + 1]
+            )
+            turned = psum.tile([P, PACK, C], F32, name="turned", tag="turned")
+            for t in range(PACK):
+                nc.tensor.transpose(turned[:, t, :], dh_sb[:, t, :], ident[:])
+            da3 = work.tile([P, C, PACK], F32, name="da3")
+            da_bf = work.tile([P, 2, C, PACK], BF16, name="da_bf", align_bytes=64)
+            nc.vector.tensor_tensor(da3[:], turned[:].rearrange("q t s -> q s t"), sig[:], MULT)
+            nc.vector.tensor_tensor(da_bf[:, 0], da3[:], slope[:], MULT)
+            nc.scalar.copy(da_bf[:, 1], da3[:])
+            da_mx[e] = quantize(da_bf[:].rearrange("q m s t -> q (m s t)"), 2 * C, "da", E)
+
+        w13_mx = {}
+
+        def prepare_w13(e):
+            grouped = work.tile([P, 2, K, PACK], BF16, name="w13_bf", align_bytes=64)
+            nc.scalar.copy(
+                grouped[:].rearrange("q m (c i) t -> q m c t i", i=4),
+                w13_raw[e][:].rearrange("q m t (c i) -> q m c t i", i=4),
+            )
+            w13_mx[e] = quantize(grouped[:].rearrange("q m k t -> q (m k t)"), 2 * K, "w13", 3)
+
+        def second(e):
+            w_codes, w_plane = w13_mx[e]
+            da_codes, da_plane = da_mx[e]
+            dx_ps = psum.tile([P, C], F32, name="dx_ps", tag="dx_ps")
+            for m in range(2):
+                nc.tensor.matmul_mx(
+                    out=dx_ps[:],
+                    lhsT=w_codes[:, m * K : (m + 1) * K].bitcast(FP8X4),
+                    lhsT_scale=w_plane[:, m * K : (m + 1) * K],
+                    rhs=da_codes[:, m * C : (m + 1) * C].bitcast(FP8X4),
+                    rhs_scale=da_plane[:, m * C : (m + 1) * C],
+                    start=(m == 0),
+                    stop=(m == 1),
+                )
+            dx_sb = work.tile([P, C], F32, name="dx_sb")
+            nc.scalar.copy(dx_sb[:], dx_ps[:])
+            nc.vector.tensor_copy(window[:].indirect(offsets[:, e * C // 16 : (e + 1) * C // 16]), dx_sb[:])
+
+        load_dy(0)
+        load_a(a1_sb, a1)
+        load_dy(1)
+        load_dy(2)
+        gather_words(0)
+        nc.vector.tensor_copy(g_plane[:], dy_plane[:].indirect(offsets[:]))
+        turn_gate()
+        for e in range(E):
+            for o in range(PASSES):
+                load_w2(e, o)
+                if (e, o) == (0, 0):
+                    load_a(a3_sb, a3)
+            if 1 <= e <= EARLY:
+                load_w13(e - 1)
+            for o in range(PASSES):
+                if e == 0 and o > 0:
+                    gather_words(o)
+                first_pass(e, o)
+            make_factors(e)
+            middle(e)
+            if 1 <= e <= EARLY:
+                prepare_w13(e - 1)
+                second(e - 1)
+        for e in range(EARLY, E):
+            load_w13(e)
+        for e in range(EARLY, E):
+            prepare_w13(e)
+            second(e)
+        nc.sync.dma_start(out, window[:])

@@ -16,6 +16,7 @@ U8 = mybir.dt.uint8
 FP8X4 = mybir.dt.float8_e4m3fn_x4
 ACT = mybir.ActivationFunctionType
 MULT = mybir.AluOpType.mult
+SUB = mybir.AluOpType.subtract
 
 P = 128
 PACK = 4
@@ -23,8 +24,29 @@ K_PASS = P * PACK
 PASSES = N // K_PASS
 RING = 12
 SCALAR_COLS = 320
-SCALAR_COLS_LAST = 192
-EARLY = 2
+SCALAR_COLS_LATE = 224
+SCALAR_COLS_LAST = 96
+HALF = H // 2
+EARLY = 4
+A_LATE = 1
+A_FIRST = 1
+T_DH = 1
+T_DA = 2
+T_DX = 0
+W13_AT = 3
+LATE_FROM = 18
+C_ACT_FROM = 5
+DA_FREE_FROM = 4
+Q_FIRST = 1
+S2_AT = 4
+W13V = 0
+Q_SAME = 0
+T_DH4 = 2
+T_DAQ = 2
+T_DAQ4 = 2
+BF = 5
+MERGE = 0
+W13SPLIT = 0
 
 
 def tile_moe_bdx_glu_sigmoid_kernel(
@@ -33,7 +55,7 @@ def tile_moe_bdx_glu_sigmoid_kernel(
     nc = tc.nc
     with ExitStack() as ctx:
         held = ctx.enter_context(tc.tile_pool(name="held", bufs=1))
-        ring = ctx.enter_context(tc.tile_pool(name="ring", bufs=RING))
+        ring = ctx.enter_context(tc.tile_pool(name="ring", bufs=1))
         work = ctx.enter_context(tc.tile_pool(name="work", bufs=2))
         psum = ctx.enter_context(tc.psum_pool(name="psum", bufs=2))
 
@@ -47,57 +69,73 @@ def tile_moe_bdx_glu_sigmoid_kernel(
             )
         gate_row = held.tile([E, C], F32, name="gate_row")
         nc.scalar.dma_start(gate_row[:], gate[0:1, :].rearrange("o (e c) -> (o e) c", e=E))
-
-        dy_plane = held.tile([P, T], U8, name="dy_plane", align_bytes=64)
-        nc.vector.memset(dy_plane[:].bitcast(I32), 0)
-        for q in range(4):
-            live = slice(32 * q, 32 * q + 4 * PASSES)
-            nc.vector.tensor_copy(dy_plane[live, :].bitcast(I32), scale_rows[live, :])
         gate_rows = held.tile([P, C], F32, name="gate_rows")
         nc.gpsimd.memset(gate_rows[:], 0.0)
         ident = held.tile([P, P], F32, name="ident")
         make_identity(nc, ident[:])
+        nc.gpsimd.tensor_copy(gate_rows[0:E, :], gate_row[:])
         window = held.tile([P, T], F32, name="window")
-        nc.gpsimd.memset(window[:], 0.0)
-        nc.vector.tensor_copy(gate_rows[0:E, :], gate_row[:])
+        nc.vector.memset(window[:], 0.0)
 
         dy_tiles = {}
         w2_raw = {}
         w13_raw = {}
+        slot_of = {}
+
+        def take_slot(key):
+            slot_of[key] = "slot%d" % (len(slot_of) % RING)
+            return slot_of[key]
 
         def load_dy(o):
-            dy_tiles[o] = held.tile([P, T], I32, name="dy%d" % o, align_bytes=64)
+            dy_tiles[o] = held.tile([P, T], I32, name="dy%d" % o, tag="dy%d" % o, align_bytes=64)
             nc.sync.dma_start(dy_tiles[o][:], dy_words[o].rearrange("p n t -> p (n t)").bitcast(I32))
 
         def load_w2(e, o):
-            w2_raw[e, o] = ring.tile([P, PACK, H], F32, name="w2_raw", tag="raw")
+            w2_raw[e, o] = ring.tile([P, PACK, H], F32, name="w2_raw", tag=take_slot((e, o)))
             nc.sync.dma_start(
                 w2_raw[e, o][:], w2[e, o * K_PASS : (o + 1) * K_PASS, :].rearrange("(p j) i -> p j i", j=PACK)
             )
 
+        def load_w2_half(h):
+            w2_raw[h] = ring.tile([P, PACK, HALF], F32, name="w2_half", tag=take_slot(("half", h)))
+            nc.sync.dma_start(
+                w2_raw[h][:],
+                w2[E - 1, N - K_PASS :, h * HALF : (h + 1) * HALF].rearrange("(p j) i -> p j i", j=PACK),
+            )
+
         def load_w13(e):
-            w13_raw[e] = ring.tile([P, 2, PACK, K], F32, name="w13_raw", tag="raw")
+            w13_raw[e] = ring.tile([P, 2, PACK, K], F32, name="w13_raw", tag=take_slot(e))
             for m, w in enumerate((w1, w3)):
                 nc.sync.dma_start(w13_raw[e][:, m], w[e].rearrange("(q t) k -> q t k", t=PACK))
 
-        a1_sb = held.tile([P, PACK, S], F32, name="a1_sb")
-        a3_sb = held.tile([P, PACK, S], F32, name="a3_sb")
+        S0 = S - A_LATE * C
+        a1_sb = held.tile([P, PACK, S0], F32, name="a1_sb")
+        a3_sb = held.tile([P, PACK, S0], F32, name="a3_sb")
 
         def load_a(tile, a):
-            nc.sync.dma_start(tile[:], a.rearrange("(q t) s -> q t s", t=PACK))
+            nc.sync.dma_start(tile[:], a[:, :S0].rearrange("(q t) s -> q t s", t=PACK))
+
+        def load_a_late():
+            for name, a in (("a1", a1), ("a3", a3)):
+                a_late[name] = ring.tile([P, PACK, A_LATE * C], F32, name="a_late", tag=take_slot(name))
+                nc.sync.dma_start(a_late[name][:], a[:, S0:].rearrange("(q t) s -> q t s", t=PACK))
+
+        a_late = {}
 
         g_words = {}
-        g_plane = held.tile([P, S], U8, name="g_plane", align_bytes=64)
 
         def gather_words(o):
             g_words[o] = held.tile([P, S], U32, name="g_words%d" % o, align_bytes=64)
             nc.vector.tensor_copy(g_words[o][:], dy_tiles[o][:].bitcast(U32).indirect(offsets[:]))
 
+        def words_walk(dst):
+            return dst.rearrange("p (c i) j -> p c j i", i=4)
+
+        def rows_walk(src):
+            return src.rearrange("p j (c i) -> p c j i", i=4)
+
         def interleave(engine_copy, dst, src):
-            engine_copy(
-                dst.rearrange("p (c i) j -> p c j i", i=4),
-                src.rearrange("p j (c i) -> p c j i", i=4),
-            )
+            engine_copy(words_walk(dst), rows_walk(src))
 
         def quantize(grouped, words, tag, bufs):
             codes = work.tile([P, words], U32, name=tag + "_codes", tag=tag + "_codes", bufs=bufs, align_bytes=64)
@@ -108,76 +146,126 @@ def tile_moe_bdx_glu_sigmoid_kernel(
         gate_cols = held.tile([P, E], F32, name="gate_cols")
 
         def turn_gate():
-            gate_ps = psum.tile([P, P], F32, name="gate_ps", tag="dx_ps")
+            gate_ps = psum.tile([P, P], F32, name="gate_ps", tag="dx_ps", bufs=3)
             nc.tensor.transpose(gate_ps[:], gate_rows[:], ident[:])
-            nc.vector.tensor_copy(gate_cols[:], gate_ps[:, 0:E])
+            nc.scalar.activation(gate_cols[:], gate_ps[:, 0:E], ACT.Copy, scale=-1.0)
 
         dh_ps = {}
+        w2_mx = {}
 
-        def first_pass(e, o):
-            grouped = work.tile([P, H, PACK], BF16, name="w2_bf", bufs=3, align_bytes=64)
+        w2_bf = {}
+
+        def cast_w2(e, o):
+            grouped = work.tile([P, H, PACK], BF16, name="w2_bf", tag="bf%d" % ((e * PASSES + o) % BF), bufs=1, align_bytes=64)
             raw = w2_raw[e, o]
-            cut = SCALAR_COLS_LAST if (e, o) == (E - 1, PASSES - 1) else SCALAR_COLS
+            cut = SCALAR_COLS_LATE if e * PASSES + o >= LATE_FROM else SCALAR_COLS
             interleave(nc.scalar.copy, grouped[:, :cut, :], raw[:, :, :cut])
             interleave(nc.vector.tensor_copy, grouped[:, cut:, :], raw[:, :, cut:])
-            codes, plane = quantize(grouped[:].rearrange("p i j -> p (i j)"), H, "w2", 4)
+            w2_bf[e, o] = grouped
+
+        def first_pass(e, o):
+            codes, plane = quantize(w2_bf[e, o][:].rearrange("p i j -> p (i j)"), H, "w2", 4)
+            w2_mx[e, o] = codes
+            width = H if e < E - 1 else HALF
+            for h in range(H // width):
+                cols = slice(h * width, (h + 1) * width)
+                first_product(e, o, h, codes[:, cols], plane[:, cols])
+
+        def first_product(e, o, h, codes, plane):
             if o == 0:
-                dh_ps[e] = psum.tile([P, H], F32, name="dh_ps", tag="dh_ps")
+                dh_ps[e, h] = psum.tile([P, codes.shape[1]], F32, name="dh_ps", tag="dh_ps", bufs=3)
             slots = slice(e * C, (e + 1) * C)
             nc.tensor.matmul_mx(
-                out=dh_ps[e][:],
+                out=dh_ps[e, h][:],
                 lhsT=g_words[o][:, slots].bitcast(FP8X4),
                 lhsT_scale=g_plane[4 * o :, slots],
-                rhs=codes[:].bitcast(FP8X4),
-                rhs_scale=plane[:],
+                rhs=codes.bitcast(FP8X4),
+                rhs_scale=plane,
                 start=(o == 0),
                 stop=(o == PASSES - 1),
             )
+
+        def last_half(h):
+            grouped = work.tile([P, HALF, PACK], BF16, name="half_bf", align_bytes=64)
+            raw = w2_raw[h]
+            cut = SCALAR_COLS_LAST
+            interleave(nc.scalar.copy, grouped[:, :cut, :], raw[:, :, :cut])
+            interleave(nc.vector.tensor_copy, grouped[:, cut:, :], raw[:, :, cut:])
+            codes, plane = quantize(grouped[:].rearrange("p i j -> p (i j)"), HALF, "half", 2)
+            w2_mx["half", h] = codes
+            first_product(E - 1, PASSES - 1, h, codes[:], plane[:])
 
         factors = {}
 
         def make_factors(e):
             slots = slice(e * C, (e + 1) * C)
-            sig = work.tile([P, C, PACK], F32, name="sig", bufs=E)
-            slope = work.tile([P, C, PACK], F32, name="slope", bufs=E)
-            a1_e = a1_sb[:, :, slots].rearrange("q t s -> q s t")
+            sig = work.tile([P, PACK, C], F32, name="sig", bufs=E)
+            slope = work.tile([P, PACK, C], F32, name="slope", bufs=E)
+            a1_e = a1_sb[:, :, slots] if e * C < S0 else a_late["a1"][:, :, e * C - S0 : (e + 1) * C - S0]
+            a3_e = a3_sb[:, :, slots] if e * C < S0 else a_late["a3"][:, :, e * C - S0 : (e + 1) * C - S0]
             nc.scalar.activation(sig[:], a1_e, ACT.Sigmoid)
-            nc.scalar.activation(slope[:], a1_e, ACT.Sigmoid, scale=-1.0)
-            nc.vector.tensor_tensor(slope[:], slope[:], a3_sb[:, :, slots].rearrange("q t s -> q s t"), MULT)
+            nc.vector.scalar_tensor_tensor(slope[:], sig[:], 1.0, a3_e, SUB, MULT)
             factors[e] = (sig, slope)
 
         da_mx = {}
 
-        def middle(e):
-            sig, slope = factors[e]
-            dh_sb = work.tile([P, PACK, P], F32, name="dh_sb")
-            nc.scalar.activation(
-                dh_sb[:], dh_ps[e][:].rearrange("s (q t) -> s t q", t=PACK), ACT.Copy, scale=gate_cols[:, e : e + 1]
-            )
-            turned = psum.tile([P, PACK, C], F32, name="turned", tag="turned")
+        turned = {}
+        da_bf = {}
+
+        def tile_behind(key, shape, name):
+            if key in slot_of:
+                return ring.tile(shape, F32, name=name, tag=slot_of[key])
+            return work.tile(shape, F32, name=name, tag=name, bufs=3)
+
+        def key_after(e, k):
+            return divmod(e * PASSES + PASSES - 1 + k, PASSES) if k else None
+
+        def turn_dh(e):
+            dh_sb = tile_behind(key_after(e, T_DH if e < E - 2 else T_DH4), [P, PACK, P], "dh_sb")
+            parts = 1 if e < E - 1 else 2
+            for h in range(parts):
+                nc.scalar.activation(
+                    dh_sb[:, :, h * P // parts : (h + 1) * P // parts],
+                    dh_ps[e, h][:].rearrange("s (q t) -> s t q", t=PACK),
+                    ACT.Copy,
+                    scale=gate_cols[:, e : e + 1],
+                )
+            turned[e] = psum.tile([P, PACK, C], F32, name="turned", tag="turned")
             for t in range(PACK):
-                nc.tensor.transpose(turned[:, t, :], dh_sb[:, t, :], ident[:])
-            da3 = work.tile([P, C, PACK], F32, name="da3")
-            da_bf = work.tile([P, 2, C, PACK], BF16, name="da_bf", align_bytes=64)
-            nc.vector.tensor_tensor(da3[:], turned[:].rearrange("q t s -> q s t"), sig[:], MULT)
-            nc.vector.tensor_tensor(da_bf[:, 0], da3[:], slope[:], MULT)
-            nc.scalar.copy(da_bf[:, 1], da3[:])
-            da_mx[e] = quantize(da_bf[:].rearrange("q m s t -> q (m s t)"), 2 * C, "da", E)
+                nc.tensor.transpose(turned[e][:, t, :], dh_sb[:, t, :], ident[:])
+
+        def make_da(e):
+            sig, slope = factors[e]
+            k = T_DAQ if e < E - 2 else T_DAQ4
+            if e < E - 1 and k:
+                da3 = work.tile([P, PACK, C], F32, name="da3", tag="bf%d" % ((e * PASSES + PASSES - 1 + k) % BF), bufs=1, align_bytes=64)
+            else:
+                da3 = work.tile([P, PACK, C], F32, name="da3", bufs=3)
+            da_bf[e] = work.tile([P, 2, C, PACK], BF16, name="da_bf", align_bytes=64)
+            nc.vector.tensor_tensor(da3[:], turned[e][:], sig[:], MULT)
+            nc.vector.tensor_tensor(words_walk(da_bf[e][:, 0]), rows_walk(da3[:]), rows_walk(slope[:]), MULT)
+            if e >= C_ACT_FROM:
+                nc.scalar.activation(words_walk(da_bf[e][:, 1]), rows_walk(da3[:]), ACT.Copy, scale=-1.0)
+            else:
+                nc.vector.tensor_scalar_mul(words_walk(da_bf[e][:, 1]), rows_walk(da3[:]), -1.0)
+
+        def quantize_da(e):
+            da_mx[e] = quantize(da_bf[e][:].rearrange("q m s t -> q (m s t)"), 2 * C, "da", E)
 
         w13_mx = {}
 
         def prepare_w13(e):
-            grouped = work.tile([P, 2, K, PACK], BF16, name="w13_bf", align_bytes=64)
-            nc.scalar.copy(
-                grouped[:].rearrange("q m (c i) t -> q m c t i", i=4),
-                w13_raw[e][:].rearrange("q m t (c i) -> q m c t i", i=4),
-            )
+            grouped = work.tile([P, 2, K, PACK], BF16, name="w13_bf", bufs=3, align_bytes=64)
+            for m in range(2):
+                interleave(nc.vector.tensor_copy if (e >= EARLY and m < W13V) else nc.scalar.copy, grouped[:, m], w13_raw[e][:, m])
             w13_mx[e] = quantize(grouped[:].rearrange("q m k t -> q (m k t)"), 2 * K, "w13", 3)
+
+        dx = {}
 
         def second(e):
             w_codes, w_plane = w13_mx[e]
             da_codes, da_plane = da_mx[e]
-            dx_ps = psum.tile([P, C], F32, name="dx_ps", tag="dx_ps")
+            dx_ps = psum.tile([P, C], F32, name="dx_ps", tag="dx_ps", bufs=3)
             for m in range(2):
                 nc.tensor.matmul_mx(
                     out=dx_ps[:],
@@ -188,36 +276,88 @@ def tile_moe_bdx_glu_sigmoid_kernel(
                     start=(m == 0),
                     stop=(m == 1),
                 )
-            dx_sb = work.tile([P, C], F32, name="dx_sb")
+            dx_sb = tile_behind(key_after(e, T_DX) if e < EARLY else None, [P, C], "dx_sb")
             nc.scalar.copy(dx_sb[:], dx_ps[:])
-            nc.vector.tensor_copy(window[:].indirect(offsets[:, e * C // 16 : (e + 1) * C // 16]), dx_sb[:])
+            dx[e] = dx_sb
+
+        done = {}
+
+        def scatter(e):
+            done[e] = 1
+            nc.vector.tensor_copy(window[:].indirect(offsets[:, e * C // 16 : (e + 1) * C // 16]), dx[e][:])
 
         load_dy(0)
-        load_a(a1_sb, a1)
         load_dy(1)
+        load_a(a1_sb, a1)
         load_dy(2)
         gather_words(0)
+        gather_words(1)
+        dy_plane = held.tile([P, T], U8, name="dy_plane", tag="dy1", align_bytes=64)
+        nc.vector.memset(dy_plane[:].bitcast(I32), 0)
+        for q in range(4):
+            live = slice(32 * q, 32 * q + 4 * PASSES)
+            nc.vector.tensor_copy(dy_plane[live, :].bitcast(I32), scale_rows[live, :])
+        g_plane = held.tile([P, S], U8, name="g_plane", align_bytes=64)
         nc.vector.tensor_copy(g_plane[:], dy_plane[:].indirect(offsets[:]))
         turn_gate()
-        for e in range(E):
-            for o in range(PASSES):
+        def due(step, lag):
+            e, o = divmod(step - lag - (PASSES - 1), PASSES)
+            return e if o == 0 and e >= 0 else None
+
+        for step in range(E * PASSES):
+            e, o = divmod(step, PASSES)
+            if step < E * PASSES - 1:
                 load_w2(e, o)
-                if (e, o) == (0, 0):
+                if step == 0:
                     load_a(a3_sb, a3)
-            if 1 <= e <= EARLY:
-                load_w13(e - 1)
-            for o in range(PASSES):
-                if e == 0 and o > 0:
-                    gather_words(o)
+                if due(step, W13_AT) is not None and due(step, W13_AT) < EARLY:
+                    load_w13(due(step, W13_AT))
+                if step == 2:
+                    gather_words(2)
+                cast_w2(e, o)
+            if Q_SAME and step < E * PASSES - 1:
                 first_pass(e, o)
-            make_factors(e)
-            middle(e)
-            if 1 <= e <= EARLY:
-                prepare_w13(e - 1)
-                second(e - 1)
+            if Q_FIRST and step >= 1 and not Q_SAME:
+                first_pass(*divmod(step - 1, PASSES))
+            if o == 1 and e >= 1 and Q_SAME:
+                turn_dh(e - 1)
+            if o == 2 and e >= 1:
+                make_da(e - 1)
+            if due(step, S2_AT + 2) is not None and due(step, S2_AT + 2) < EARLY:
+                scatter(due(step, S2_AT + 2))
+            if not Q_FIRST and step >= 1 and not Q_SAME:
+                first_pass(*divmod(step - 1, PASSES))
+            if o == 1 and e >= 1 and not Q_SAME:
+                turn_dh(e - 1)
+            if o == 0 and e >= 2:
+                quantize_da(e - 2)
+            if due(step, S2_AT) is not None and due(step, S2_AT) < EARLY:
+                prepare_w13(due(step, S2_AT))
+            if due(step, S2_AT + 1) is not None and due(step, S2_AT + 1) < EARLY:
+                second(due(step, S2_AT + 1))
+            if o == 0 and e >= 1:
+                make_factors(e - 1)
+        for h in range(2):
+            load_w2_half(h)
+        if A_LATE and A_FIRST:
+            load_a_late()
         for e in range(EARLY, E):
             load_w13(e)
-        for e in range(EARLY, E):
-            prepare_w13(e)
-            second(e)
+            if A_LATE and not A_FIRST and e == EARLY:
+                load_a_late()
+        for h in range(2):
+            last_half(h)
+        quantize_da(E - 2)
+        turn_dh(E - 1)
+        make_factors(E - 1)
+        make_da(E - 1)
+        quantize_da(E - 1)
+        for e in range(E):
+            if e not in w13_mx:
+                prepare_w13(e)
+        for e in range(E):
+            if e not in dx:
+                second(e)
+            if e not in done:
+                scatter(e)
         nc.sync.dma_start(out, window[:])

@@ -32,13 +32,13 @@ A_LATE = 1
 A_FIRST = 1
 T_DH = 1
 T_DA = 2
-T_DX = 0
+T_DX = 5
 W13_AT = 3
 LATE_FROM = 18
 C_ACT_FROM = 5
 DA_FREE_FROM = 4
 Q_FIRST = 1
-S2_AT = 4
+S2_AT = 5
 W13V = 0
 Q_SAME = 0
 T_DH4 = 2

from contextlib import ExitStack

import concourse.mybir as mybir
from concourse.masks import make_identity

K, T, E, C, H, N = 128, 1024, 6, 128, 512, 1536
S = E * C
FLOPS = 2 * S * (N * H + 2 * H * K)

F32 = mybir.dt.float32
BF16 = mybir.dt.bfloat16
I32 = mybir.dt.int32
U32 = mybir.dt.uint32
U16 = mybir.dt.uint16
U8 = mybir.dt.uint8
FP8X4 = mybir.dt.float8_e4m3fn_x4
ACT = mybir.ActivationFunctionType
MULT = mybir.AluOpType.mult
SUB = mybir.AluOpType.subtract

P = 128
PACK = 4
K_PASS = P * PACK
PASSES = N // K_PASS
RING = 12
SCALAR_COLS = 320
SCALAR_COLS_LATE = 224
SCALAR_COLS_LAST = 96
HALF = H // 2
EARLY = 4
A_LATE = 1
A_FIRST = 1
T_DH = 1
T_DA = 2
T_DX = 5
W13_AT = 3
LATE_FROM = 18
C_ACT_FROM = 5
DA_FREE_FROM = 4
Q_FIRST = 1
S2_AT = 5
W13V = 0
Q_SAME = 0
T_DH4 = 2
T_DAQ = 2
T_DAQ4 = 2
BF = 5
MERGE = 0
W13SPLIT = 0


def tile_moe_bdx_glu_sigmoid_kernel(
    tc, dy_words, dy_scales, a1, a3, w2, w1, w3, gate, offs, out
):
    nc = tc.nc
    with ExitStack() as ctx:
        held = ctx.enter_context(tc.tile_pool(name="held", bufs=1))
        ring = ctx.enter_context(tc.tile_pool(name="ring", bufs=1))
        work = ctx.enter_context(tc.tile_pool(name="work", bufs=2))
        psum = ctx.enter_context(tc.psum_pool(name="psum", bufs=2))

        offsets = held.tile([P, S // 16], U16, name="offsets")
        nc.sync.dma_start(offsets[:], offs)

        scale_rows = held.tile([P, T // 4], I32, name="scale_rows")
        for q in range(4):
            nc.scalar.dma_start(
                scale_rows[32 * q : 32 * q + 4 * PASSES, :], dy_scales[:, 4 * q : 4 * q + 4, :].bitcast(I32)
            )
        gate_row = held.tile([E, C], F32, name="gate_row")
        nc.scalar.dma_start(gate_row[:], gate[0:1, :].rearrange("o (e c) -> (o e) c", e=E))
        gate_rows = held.tile([P, C], F32, name="gate_rows")
        nc.gpsimd.memset(gate_rows[:], 0.0)
        ident = held.tile([P, P], F32, name="ident")
        make_identity(nc, ident[:])
        nc.gpsimd.tensor_copy(gate_rows[0:E, :], gate_row[:])
        window = held.tile([P, T], F32, name="window")
        nc.vector.memset(window[:], 0.0)

        dy_tiles = {}
        w2_raw = {}
        w13_raw = {}
        slot_of = {}

        def take_slot(key):
            slot_of[key] = "slot%d" % (len(slot_of) % RING)
            return slot_of[key]

        def load_dy(o):
            dy_tiles[o] = held.tile([P, T], I32, name="dy%d" % o, tag="dy%d" % o, align_bytes=64)
            nc.sync.dma_start(dy_tiles[o][:], dy_words[o].rearrange("p n t -> p (n t)").bitcast(I32))

        def load_w2(e, o):
            w2_raw[e, o] = ring.tile([P, PACK, H], F32, name="w2_raw", tag=take_slot((e, o)))
            nc.sync.dma_start(
                w2_raw[e, o][:], w2[e, o * K_PASS : (o + 1) * K_PASS, :].rearrange("(p j) i -> p j i", j=PACK)
            )

        def load_w2_half(h):
            w2_raw[h] = ring.tile([P, PACK, HALF], F32, name="w2_half", tag=take_slot(("half", h)))
            nc.sync.dma_start(
                w2_raw[h][:],
                w2[E - 1, N - K_PASS :, h * HALF : (h + 1) * HALF].rearrange("(p j) i -> p j i", j=PACK),
            )

        def load_w13(e):
            w13_raw[e] = ring.tile([P, 2, PACK, K], F32, name="w13_raw", tag=take_slot(e))
            for m, w in enumerate((w1, w3)):
                nc.sync.dma_start(w13_raw[e][:, m], w[e].rearrange("(q t) k -> q t k", t=PACK))

        S0 = S - A_LATE * C
        a1_sb = held.tile([P, PACK, S0], F32, name="a1_sb")
        a3_sb = held.tile([P, PACK, S0], F32, name="a3_sb")

        def load_a(tile, a):
            nc.sync.dma_start(tile[:], a[:, :S0].rearrange("(q t) s -> q t s", t=PACK))

        def load_a_late():
            for name, a in (("a1", a1), ("a3", a3)):
                a_late[name] = ring.tile([P, PACK, A_LATE * C], F32, name="a_late", tag=take_slot(name))
                nc.sync.dma_start(a_late[name][:], a[:, S0:].rearrange("(q t) s -> q t s", t=PACK))

        a_late = {}

        g_words = {}

        def gather_words(o):
            g_words[o] = held.tile([P, S], U32, name="g_words%d" % o, align_bytes=64)
            nc.vector.tensor_copy(g_words[o][:], dy_tiles[o][:].bitcast(U32).indirect(offsets[:]))

        def words_walk(dst):
            return dst.rearrange("p (c i) j -> p c j i", i=4)

        def rows_walk(src):
            return src.rearrange("p j (c i) -> p c j i", i=4)

        def interleave(engine_copy, dst, src):
            engine_copy(words_walk(dst), rows_walk(src))

        def quantize(grouped, words, tag, bufs):
            codes = work.tile([P, words], U32, name=tag + "_codes", tag=tag + "_codes", bufs=bufs, align_bytes=64)
            plane = work.tile([P, words], U8, name=tag + "_plane", tag=tag + "_plane", bufs=bufs, align_bytes=64)
            nc.vector.quantize_mx(out=codes[:].bitcast(FP8X4), scales=plane[:], in_=grouped)
            return codes, plane

        gate_cols = held.tile([P, E], F32, name="gate_cols")

        def turn_gate():
            gate_ps = psum.tile([P, P], F32, name="gate_ps", tag="dx_ps", bufs=3)
            nc.tensor.transpose(gate_ps[:], gate_rows[:], ident[:])
            nc.scalar.activation(gate_cols[:], gate_ps[:, 0:E], ACT.Copy, scale=-1.0)

        dh_ps = {}
        w2_mx = {}

        w2_bf = {}

        def cast_w2(e, o):
            grouped = work.tile([P, H, PACK], BF16, name="w2_bf", tag="bf%d" % ((e * PASSES + o) % BF), bufs=1, align_bytes=64)
            raw = w2_raw[e, o]
            cut = SCALAR_COLS_LATE if e * PASSES + o >= LATE_FROM else SCALAR_COLS
            interleave(nc.scalar.copy, grouped[:, :cut, :], raw[:, :, :cut])
            interleave(nc.vector.tensor_copy, grouped[:, cut:, :], raw[:, :, cut:])
            w2_bf[e, o] = grouped

        def first_pass(e, o):
            codes, plane = quantize(w2_bf[e, o][:].rearrange("p i j -> p (i j)"), H, "w2", 4)
            w2_mx[e, o] = codes
            width = H if e < E - 1 else HALF
            for h in range(H // width):
                cols = slice(h * width, (h + 1) * width)
                first_product(e, o, h, codes[:, cols], plane[:, cols])

        def first_product(e, o, h, codes, plane):
            if o == 0:
                dh_ps[e, h] = psum.tile([P, codes.shape[1]], F32, name="dh_ps", tag="dh_ps", bufs=3)
            slots = slice(e * C, (e + 1) * C)
            nc.tensor.matmul_mx(
                out=dh_ps[e, h][:],
                lhsT=g_words[o][:, slots].bitcast(FP8X4),
                lhsT_scale=g_plane[4 * o :, slots],
                rhs=codes.bitcast(FP8X4),
                rhs_scale=plane,
                start=(o == 0),
                stop=(o == PASSES - 1),
            )

        def last_half(h):
            grouped = work.tile([P, HALF, PACK], BF16, name="half_bf", align_bytes=64)
            raw = w2_raw[h]
            cut = SCALAR_COLS_LAST
            interleave(nc.scalar.copy, grouped[:, :cut, :], raw[:, :, :cut])
            interleave(nc.vector.tensor_copy, grouped[:, cut:, :], raw[:, :, cut:])
            codes, plane = quantize(grouped[:].rearrange("p i j -> p (i j)"), HALF, "half", 2)
            w2_mx["half", h] = codes
            first_product(E - 1, PASSES - 1, h, codes[:], plane[:])

        factors = {}

        def make_factors(e):
            slots = slice(e * C, (e + 1) * C)
            sig = work.tile([P, PACK, C], F32, name="sig", bufs=E)
            slope = work.tile([P, PACK, C], F32, name="slope", bufs=E)
            a1_e = a1_sb[:, :, slots] if e * C < S0 else a_late["a1"][:, :, e * C - S0 : (e + 1) * C - S0]
            a3_e = a3_sb[:, :, slots] if e * C < S0 else a_late["a3"][:, :, e * C - S0 : (e + 1) * C - S0]
            nc.scalar.activation(sig[:], a1_e, ACT.Sigmoid)
            nc.vector.scalar_tensor_tensor(slope[:], sig[:], 1.0, a3_e, SUB, MULT)
            factors[e] = (sig, slope)

        da_mx = {}

        turned = {}
        da_bf = {}

        def tile_behind(key, shape, name):
            if key in slot_of:
                return ring.tile(shape, F32, name=name, tag=slot_of[key])
            return work.tile(shape, F32, name=name, tag=name, bufs=3)

        def key_after(e, k):
            return divmod(e * PASSES + PASSES - 1 + k, PASSES) if k else None

        def turn_dh(e):
            dh_sb = tile_behind(key_after(e, T_DH if e < E - 2 else T_DH4), [P, PACK, P], "dh_sb")
            parts = 1 if e < E - 1 else 2
            for h in range(parts):
                nc.scalar.activation(
                    dh_sb[:, :, h * P // parts : (h + 1) * P // parts],
                    dh_ps[e, h][:].rearrange("s (q t) -> s t q", t=PACK),
                    ACT.Copy,
                    scale=gate_cols[:, e : e + 1],
                )
            turned[e] = psum.tile([P, PACK, C], F32, name="turned", tag="turned")
            for t in range(PACK):
                nc.tensor.transpose(turned[e][:, t, :], dh_sb[:, t, :], ident[:])

        def make_da(e):
            sig, slope = factors[e]
            k = T_DAQ if e < E - 2 else T_DAQ4
            if e < E - 1 and k:
                da3 = work.tile([P, PACK, C], F32, name="da3", tag="bf%d" % ((e * PASSES + PASSES - 1 + k) % BF), bufs=1, align_bytes=64)
            else:
                da3 = work.tile([P, PACK, C], F32, name="da3", bufs=3)
            da_bf[e] = work.tile([P, 2, C, PACK], BF16, name="da_bf", align_bytes=64)
            nc.vector.tensor_tensor(da3[:], turned[e][:], sig[:], MULT)
            nc.vector.tensor_tensor(words_walk(da_bf[e][:, 0]), rows_walk(da3[:]), rows_walk(slope[:]), MULT)
            if e >= C_ACT_FROM:
                nc.scalar.activation(words_walk(da_bf[e][:, 1]), rows_walk(da3[:]), ACT.Copy, scale=-1.0)
            else:
                nc.vector.tensor_scalar_mul(words_walk(da_bf[e][:, 1]), rows_walk(da3[:]), -1.0)

        def quantize_da(e):
            da_mx[e] = quantize(da_bf[e][:].rearrange("q m s t -> q (m s t)"), 2 * C, "da", E)

        w13_mx = {}

        def prepare_w13(e):
            grouped = work.tile([P, 2, K, PACK], BF16, name="w13_bf", bufs=3, align_bytes=64)
            for m in range(2):
                interleave(nc.vector.tensor_copy if (e >= EARLY and m < W13V) else nc.scalar.copy, grouped[:, m], w13_raw[e][:, m])
            w13_mx[e] = quantize(grouped[:].rearrange("q m k t -> q (m k t)"), 2 * K, "w13", 3)

        dx = {}

        def second(e):
            w_codes, w_plane = w13_mx[e]
            da_codes, da_plane = da_mx[e]
            dx_ps = psum.tile([P, C], F32, name="dx_ps", tag="dx_ps", bufs=3)
            for m in range(2):
                nc.tensor.matmul_mx(
                    out=dx_ps[:],
                    lhsT=w_codes[:, m * K : (m + 1) * K].bitcast(FP8X4),
                    lhsT_scale=w_plane[:, m * K : (m + 1) * K],
                    rhs=da_codes[:, m * C : (m + 1) * C].bitcast(FP8X4),
                    rhs_scale=da_plane[:, m * C : (m + 1) * C],
                    start=(m == 0),
                    stop=(m == 1),
                )
            dx_sb = tile_behind(key_after(e, T_DX) if e < EARLY else None, [P, C], "dx_sb")
            nc.scalar.copy(dx_sb[:], dx_ps[:])
            dx[e] = dx_sb

        done = {}

        def scatter(e):
            done[e] = 1
            nc.vector.tensor_copy(window[:].indirect(offsets[:, e * C // 16 : (e + 1) * C // 16]), dx[e][:])

        load_dy(0)
        load_dy(1)
        load_a(a1_sb, a1)
        load_dy(2)
        gather_words(0)
        gather_words(1)
        dy_plane = held.tile([P, T], U8, name="dy_plane", tag="dy1", align_bytes=64)
        nc.vector.memset(dy_plane[:].bitcast(I32), 0)
        for q in range(4):
            live = slice(32 * q, 32 * q + 4 * PASSES)
            nc.vector.tensor_copy(dy_plane[live, :].bitcast(I32), scale_rows[live, :])
        g_plane = held.tile([P, S], U8, name="g_plane", align_bytes=64)
        nc.vector.tensor_copy(g_plane[:], dy_plane[:].indirect(offsets[:]))
        turn_gate()
        def due(step, lag):
            e, o = divmod(step - lag - (PASSES - 1), PASSES)
            return e if o == 0 and e >= 0 else None

        for step in range(E * PASSES):
            e, o = divmod(step, PASSES)
            if step < E * PASSES - 1:
                load_w2(e, o)
                if step == 0:
                    load_a(a3_sb, a3)
                if due(step, W13_AT) is not None and due(step, W13_AT) < EARLY:
                    load_w13(due(step, W13_AT))
                if step == 2:
                    gather_words(2)
                cast_w2(e, o)
            if Q_SAME and step < E * PASSES - 1:
                first_pass(e, o)
            if Q_FIRST and step >= 1 and not Q_SAME:
                first_pass(*divmod(step - 1, PASSES))
            if o == 1 and e >= 1 and Q_SAME:
                turn_dh(e - 1)
            if o == 2 and e >= 1:
                make_da(e - 1)
            if due(step, S2_AT + 2) is not None and due(step, S2_AT + 2) < EARLY:
                scatter(due(step, S2_AT + 2))
            if not Q_FIRST and step >= 1 and not Q_SAME:
                first_pass(*divmod(step - 1, PASSES))
            if o == 1 and e >= 1 and not Q_SAME:
                turn_dh(e - 1)
            if o == 0 and e >= 2:
                quantize_da(e - 2)
            if due(step, S2_AT) is not None and due(step, S2_AT) < EARLY:
                prepare_w13(due(step, S2_AT))
            if due(step, S2_AT + 1) is not None and due(step, S2_AT + 1) < EARLY:
                second(due(step, S2_AT + 1))
            if o == 0 and e >= 1:
                make_factors(e - 1)
        for h in range(2):
            load_w2_half(h)
        if A_LATE and A_FIRST:
            load_a_late()
        for e in range(EARLY, E):
            load_w13(e)
            if A_LATE and not A_FIRST and e == EARLY:
                load_a_late()
        for h in range(2):
            last_half(h)
        quantize_da(E - 2)
        turn_dh(E - 1)
        make_factors(E - 1)
        make_da(E - 1)
        quantize_da(E - 1)
        for e in range(E):
            if e not in w13_mx:
                prepare_w13(e)
        for e in range(E):
            if e not in dx:
                second(e)
            if e not in done:
                scatter(e)
        nc.sync.dma_start(out, window[:])
